import numpy as np
import ml_dtypes


def mxq(x, axis, fmt="e4m3"):
    dtype, down = {"e4m3": (ml_dtypes.float8_e4m3fn, 7), "e5m2": (ml_dtypes.float8_e5m2, 14)}[fmt]
    v = np.moveaxis(np.asarray(x, np.float32).astype(ml_dtypes.bfloat16).astype(np.float64), axis, -1)
    blocks = v.reshape(v.shape[:-1] + (-1, 32))
    amax = np.abs(blocks).max(-1, keepdims=True)
    byte = np.maximum(np.where(amax > 0, np.frexp(amax)[1] - 1 + 127, 0) - down, 1)
    scale = np.exp2(byte - 127.0)
    codes = (blocks / scale).astype(np.float32).astype(dtype).astype(np.float64)
    return np.moveaxis((codes * scale).reshape(v.shape), -1, axis)


WIDE = False


def mx_kscale(k):
    if not WIDE:
        return np.ones(k)
    levels = np.array([10, -10, 5, -5, 0])
    if k % 512:
        return np.exp2(np.random.permutation(np.resize(levels, k // 32))).repeat(32)
    a = np.empty((k // 512, 16))
    for p in range(k // 512):
        a[p, :8] = np.random.permutation(np.resize(levels, 8))
        for g in range(8):
            far = levels[np.abs(levels - a[p, g]) >= 10]
            a[p, g + 8] = far[np.random.randint(len(far))]
    return np.exp2(a.ravel()).repeat(32)


def f64(x):
    return np.asarray(x).astype(np.float64)


def striped(idx):
    return np.tile(idx.reshape(-1, 16).T, (8, 1)).astype(np.uint16)


def unstriped(offs):
    return offs[:16].T.reshape(-1).astype(np.int64)


def pack_weight(w):
    k, n = w.shape
    w = f64(np.asarray(w, np.float32).astype(ml_dtypes.bfloat16)).reshape(k // 32, 32, n)
    amax = np.abs(w).max(1)
    byte = np.clip(np.where(amax > 0, np.frexp(amax)[1] - 1 + 127 - 7, 1), 1, 254)
    scaled = (w * np.exp2(127.0 - byte)[:, None, :]).reshape(k, n).astype(np.float32)
    words = np.ascontiguousarray(scaled.reshape(k // 512, 128, 4, n).transpose(0, 1, 3, 2)).astype(ml_dtypes.float8_e4m3fn).view(np.uint8)
    return words, np.ascontiguousarray(byte.astype(np.uint8).reshape(k // 512, 16, n))


def unpack_weight(words, scales):
    g, p, n, _ = words.shape
    vals = np.ascontiguousarray(words).view(ml_dtypes.float8_e4m3fn).astype(np.float64) * np.repeat(np.exp2(scales.astype(np.float64) - 127.0), 8, axis=1)[..., None]
    return vals.transpose(0, 1, 3, 2).reshape(g * 512, n)


E2M1 = np.array([0.0, 0.5, 1.0, 1.5, 2.0, 3.0, 4.0, 6.0, -0.0, -0.5, -1.0, -1.5, -2.0, -3.0, -4.0, -6.0])


def pack_fp4(w):
    k, n = w.shape
    w = f64(np.asarray(w, np.float32).astype(ml_dtypes.bfloat16)).reshape(k // 32, 32, n)
    amax = np.abs(w).max(1)
    mant, ex = np.frexp(amax / 6.0)
    byte = np.clip(np.where(amax > 0, np.where(mant > 0.5, ex, ex - 1) + 127, 1), 1, 254)
    scaled = (w * np.exp2(127.0 - byte)[:, None, :]).reshape(k, n).astype(np.float32)
    c = np.ascontiguousarray(scaled.reshape(k // 512, 128, 4, n).transpose(0, 1, 3, 2)).astype(ml_dtypes.float4_e2m1fn).view(np.uint8) & 0xF
    words = (c[..., 0::2] | (c[..., 1::2] << 4)).reshape(k // 512, 128, 2 * n)
    return np.ascontiguousarray(words), np.ascontiguousarray(byte.astype(np.uint8).reshape(k // 512, 16, n))


def unpack_fp4(words, scales):
    g, _, n = scales.shape
    words = np.ascontiguousarray(words).reshape(g, 128, n, 2)
    nib = np.empty((g, 128, n, 4), np.uint8)
    nib[..., 0::2] = words & 0xF
    nib[..., 1::2] = words >> 4
    vals = E2M1[nib] * np.repeat(np.exp2(scales.astype(np.float64) - 127.0), 8, axis=1)[..., None]
    return vals.transpose(0, 1, 3, 2).reshape(g * 512, n)


def planes(y):
    n, m = y.shape
    v = y.astype(np.float32).astype(ml_dtypes.bfloat16).astype(np.float64).reshape(n // 32, 32, m)
    top = np.abs(v).max(1)
    byte = np.clip(np.where(top > 0, np.frexp(top)[1] - 1 + 127 - 7, 1), 1, 254)
    codes = (v * np.exp2(127.0 - byte)[:, None, :]).reshape(n, m).astype(np.float32).astype(ml_dtypes.float8_e4m3fn).view(np.uint8)
    words = codes.reshape(n // 512, 128, 4, m).transpose(0, 1, 3, 2)
    return np.ascontiguousarray(words), np.ascontiguousarray(byte.astype(np.uint8).reshape(n // 512, 16, m))


K, T, S, N, H, U = 1024, 2048, 512, 512, 512, 1024


def setup_inputs():
    n = np.random.standard_normal
    s = mx_kscale(K)[:, None]
    u = mx_kscale(H)
    packed_xT = pack_weight(n((K, T)) * s)
    packed_w1 = pack_fp4(n((K, N)) / np.sqrt(K) / s)
    packed_w2 = pack_fp4(n((H, N)) / np.sqrt(H) / u[:, None])
    return {
        "x_words": packed_xT[0],
        "x_scales": packed_xT[1],
        "w1_words": packed_w1[0],
        "w1_scales": packed_w1[1],
        "unit": (np.random.uniform(0.6, 1.4, (H, 1)) * u[:, None]).astype(np.float32),
        "w2_words": packed_w2[0],
        "w2_scales": packed_w2[1],
        "offs": striped(np.random.permutation(T)[:S]),
        "nu": striped(np.random.permutation(np.concatenate([np.arange(S), np.random.randint(0, S, U - S)]))),
        "el": striped(np.random.permutation(np.concatenate([np.arange(S), np.random.randint(0, S, U - S)]))),
        "ct": striped(np.random.permutation(np.concatenate([np.arange(S), np.random.randint(0, S, U - S)]))),
    }


def reference(x_words, x_scales, w1_words, w1_scales, unit, w2_words, w2_scales, offs, nu, el, ct):
    xq = unpack_weight(x_words, x_scales)[:, unstriped(offs)]
    y = unpack_fp4(w1_words, w1_scales).T @ xq
    yn = y[:, unstriped(nu)]
    ye1 = y[:, unstriped(el)]
    mxr = np.maximum(yn, ye1)
    yc2 = y[:, unstriped(ct)]
    act1 = mxr + yc2
    hid = f64(unit) * (act1 * ye1)
    out_0 = unpack_fp4(w2_words, w2_scales).T @ mxq(hid, 0, "e4m3")
    return (out_0,) + planes(out_0)

@@ -1,0 +1,178 @@
+from contextlib import ExitStack
+
+import concourse.mybir as mybir
+
+K, T, S, H, N, U = 1024, 2048, 512, 512, 512, 1024
+FLOPS = 2 * K * H * S + 2 * H * N * U
+
+F32 = mybir.dt.float32
+BF16 = mybir.dt.bfloat16
+I32 = mybir.dt.int32
+U32 = mybir.dt.uint32
+U16 = mybir.dt.uint16
+U8 = mybir.dt.uint8
+FP8X4 = mybir.dt.float8_e4m3fn_x4
+FP4X4 = mybir.dt.float4_e2m1fn_x4
+ALU = mybir.AluOpType
+ACT = mybir.ActivationFunctionType
+
+P = 128
+PACK = 4
+PASSES = K // (P * PACK)
+WIDTHS = (256, 256, 256, 128, 128)
+BANK = 512
+
+
+def tile_picked_ypartnr_max_po_kernel(
+    tc, x_words, x_scales, w1_words, w1_scales, unit, w2_words, w2_scales, offs, nu, el, ct, out_0, out_1, out_2
+):
+    nc = tc.nc
+    with ExitStack() as ctx:
+        keep = ctx.enter_context(tc.tile_pool(name="keep", bufs=1))
+        ring = ctx.enter_context(tc.tile_pool(name="ring", bufs=2))
+        psum1 = ctx.enter_context(tc.psum_pool(name="psum1", bufs=1))
+        psum2 = ctx.enter_context(tc.psum_pool(name="psum2", bufs=2))
+
+        def load_scale_rows(queues, dst, src):
+            for q, queue in enumerate(queues):
+                queue.dma_start(
+                    out=dst[32 * q : 32 * q + 4].bitcast(I32),
+                    in_=src[:, 4 * q : 4 * q + 4, :].bitcast(I32).rearrange("o r c -> r o c"),
+                )
+
+        xs = keep.tile([P, PASSES, T], U8, name="xs", align_bytes=64)
+        ws_raw = keep.tile([P, PASSES, H], U8, name="ws_raw", align_bytes=64)
+        nc.vector.memset(xs[:].bitcast(I32), 0)
+        nc.gpsimd.memset(ws_raw[:].bitcast(I32), 0)
+
+        offs_sb = keep.tile([P, S // 16], U16, name="offs_sb")
+        nc.sync.dma_start(offs_sb[:], offs)
+        xw = [keep.tile([P, T], I32, name=f"xw{o}", align_bytes=64) for o in range(PASSES)]
+        ww_raw = keep.tile([P, PASSES, 2 * H], U8, name="ww_raw", align_bytes=64)
+        nc.sync.dma_start(out=ww_raw[:].bitcast(I32), in_=w1_words.bitcast(I32).rearrange("o p c -> p o c"))
+        u_sb = keep.tile([P, PACK], F32, name="u_sb")
+        nc.sync.dma_start(out=u_sb[:], in_=unit.rearrange("(p t) o -> p (t o)", t=PACK))
+        load_scale_rows((nc.scalar, nc.scalar, nc.gpsimd, nc.gpsimd), ws_raw[:], w1_scales)
+        load_scale_rows([nc.scalar] * 4, xs[:], x_scales)
+        for o in range(PASSES):
+            nc.sync.dma_start(out=xw[o][:], in_=x_words[o].rearrange("p c t -> p (c t)").bitcast(I32))
+        lists = {}
+        for name, src in (("el", el), ("nu", nu), ("ct", ct)):
+            lists[name] = keep.tile([P, U // 16], U16, name=f"{name}_sb")
+            nc.sync.dma_start(lists[name][:], src)
+
+        sign = keep.tile([P, PACK], F32, name="sign")
+        nc.scalar.activation(sign[:], u_sb[:], ACT.Sign)
+
+        def deal(words_raw, scales_raw, name):
+            words = keep.tile([P, PACK, P, 2], U8, name=f"{name}_words", align_bytes=64)
+            scales = keep.tile([P, PACK, P], U8, name=f"{name}_scales", align_bytes=64)
+            nc.vector.tensor_copy(words[:], words_raw.rearrange("p (m t b) -> p t m b", t=PACK, b=2))
+            nc.vector.tensor_copy(scales[:], scales_raw.rearrange("p (m t) -> p t m", t=PACK))
+            return words, scales
+
+        def stationary(dealt, t):
+            words, scales = dealt
+            return dict(lhsT=words[:, t].rearrange("p m b -> p (m b)").bitcast(FP4X4), lhsT_scale=scales[:, t, :])
+
+        y_banks = [psum1.tile([P, S], F32, name=f"y{t}") for t in range(PACK)]
+        for o in range(PASSES):
+            w1 = deal(ww_raw[:, o, :], ws_raw[:, o, :], f"w1_{o}")
+            xq_s = keep.tile([P, S], U8, name=f"xq_s{o}", align_bytes=64)
+            xq_w = keep.tile([P, S], U32, name=f"xq_w{o}", align_bytes=64)
+            nc.vector.tensor_copy(xq_s[:], xs[:, o, :].indirect(offs_sb[:]))
+            nc.vector.tensor_copy(xq_w[:], xw[o][:].bitcast(U32).indirect(offs_sb[:]))
+            for t in range(PACK):
+                nc.tensor.matmul_mx(
+                    out=y_banks[t][:], rhs=xq_w[:].bitcast(FP8X4), rhs_scale=xq_s[:],
+                    start=(o == 0), stop=(o == PASSES - 1), **stationary(w1, t),
+                )
+
+        nc.sync.dma_start(out=ww_raw[:, 0:1, :].bitcast(I32), in_=w2_words.bitcast(I32).rearrange("o p c -> p o c"))
+        load_scale_rows([nc.sync] * 4, ws_raw[:, 0:1, :], w2_scales)
+        w2 = deal(ww_raw[:, 0, :], ws_raw[:, 0, :], "w2")
+
+        y_signed, y_scaled = [], []
+        for t in range(PACK):
+            ys = keep.tile([P, S], F32, name=f"y_signed{t}")
+            ya = keep.tile([P, S], F32, name=f"y_scaled{t}")
+            if t % 2 == 0:
+                nc.scalar.activation(ys[:], y_banks[t][:], ACT.Copy, scale=sign[:, t : t + 1])
+            else:
+                nc.vector.tensor_scalar(ys[:], y_banks[t][:], sign[:, t : t + 1], None, ALU.mult)
+            nc.vector.tensor_scalar(ya[:], ys[:], u_sb[:, t : t + 1], None, ALU.mult)
+            y_signed.append(ys)
+            y_scaled.append(ya)
+
+        out_scales = keep.tile([P, U], U8, name="out_scales", align_bytes=64)
+        out_rows = out_0.rearrange("(p t) r -> p t r", t=PACK)
+        out_words = out_1[0].rearrange("p c t -> p (c t)").bitcast(I32)
+
+        def woven(ap):
+            return ap.rearrange("p (c i) t -> p c t i", i=4)
+
+        def by_rows(ap):
+            return ap.rearrange("p t (c i) -> p c t i", i=4)
+
+        def hidden(r0, width):
+            cols = slice(r0 // 16, (r0 + width) // 16)
+            taker = ring.tile([P, PACK, width], F32, name="taker")
+            giver = ring.tile([P, PACK, width], F32, name="giver")
+            larger = ring.tile([P, PACK, width], F32, name="larger")
+            act = ring.tile([P, PACK, width], F32, name="act")
+            for t in range(PACK):
+                nc.scalar.activation(taker[:, t, :], y_signed[t][:].indirect(lists["el"][:, cols]), ACT.Copy)
+                nc.scalar.activation(giver[:, t, :], y_scaled[t][:].indirect(lists["nu"][:, cols]), ACT.Copy)
+            for t in range(PACK + 1):
+                if t < PACK:
+                    nc.vector.scalar_tensor_tensor(
+                        larger[:, t, :], taker[:, t, :], u_sb[:, t : t + 1], giver[:, t, :], ALU.mult, ALU.max
+                    )
+                if t > 0:
+                    nc.vector.tensor_tensor(
+                        act[:, t - 1, :], y_scaled[t - 1][:].indirect(lists["ct"][:, cols]), larger[:, t - 1, :], ALU.add
+                    )
+            hid = ring.tile([P, width, PACK], BF16, name="hid", align_bytes=64)
+            nc.vector.tensor_tensor(woven(hid[:]), by_rows(act[:]), by_rows(taker[:]), ALU.mult)
+            return hid
+
+        def second_product(hid, width):
+            codes = ring.tile([P, width], U32, name="hid_codes", align_bytes=64)
+            scales = ring.tile([P, width], U8, name="hid_scales", align_bytes=64)
+            nc.vector.quantize_mx(out=codes[:].bitcast(FP8X4), scales=scales[:], in_=hid[:].rearrange("p r t -> p (r t)"))
+            res = ring.tile([P, PACK, width], F32, name="res")
+            per_bank = min(BANK // width, PACK)
+            for b in range(PACK // per_bank):
+                bank = psum2.tile([P, per_bank, width], F32, name=f"bank{b}")
+                for j in range(per_bank):
+                    nc.tensor.matmul_mx(
+                        out=bank[:, j, :], rhs=codes[:].bitcast(FP8X4), rhs_scale=scales[:],
+                        start=True, stop=True, **stationary(w2, per_bank * b + j),
+                    )
+                nc.scalar.copy(res[:, per_bank * b : per_bank * (b + 1), :], bank[:])
+            return res
+
+        def hand_out(res, r0, width):
+            nc.sync.dma_start(out=out_rows[:, :, r0 : r0 + width], in_=res[:])
+            rounded = ring.tile([P, width, PACK], BF16, name="rounded", align_bytes=64)
+            nc.vector.tensor_copy(woven(rounded[:]), by_rows(res[:]))
+            codes = ring.tile([P, width], U32, name="out_codes", align_bytes=64)
+            nc.vector.quantize_mx(
+                out=codes[:].bitcast(FP8X4), scales=out_scales[:, r0 : r0 + width],
+                in_=rounded[:].rearrange("p r t -> p (r t)"),
+            )
+            nc.sync.dma_start(out=out_words[:, r0 : r0 + width], in_=codes[:].bitcast(I32))
+
+        waiting = None
+        r0 = 0
+        for width in WIDTHS:
+            hid = hidden(r0, width)
+            if waiting is not None:
+                hand_out(*waiting)
+            waiting = (second_product(hid, width), r0, width)
+            r0 = r0 + width
+        hand_out(*waiting)
+        for q in range(4):
+            nc.sync.dma_start(
+                out=out_2[0, 4 * q : 4 * q + 4, :].bitcast(I32), in_=out_scales[32 * q : 32 * q + 4, :].bitcast(I32)
+            )

@@ -19,8 +19,19 @@ ACT = mybir.ActivationFunctionType
 P = 128
 PACK = 4
 PASSES = K // (P * PACK)
-WIDTHS = (256, 256, 256, 128, 128)
+WIDTHS = (512, 384, 128)
+FUSED = (4, 2, 0)
+WINDOW = S + 16
 BANK = 512
+
+
+def pieces(width):
+    cuts, c0 = [], 0
+    for n in (512, 256, 128):
+        if width - c0 >= n:
+            cuts.append((c0, c0 + n))
+            c0 = c0 + n
+    return cuts
 
 
 def tile_picked_ypartnr_max_po_kernel(
@@ -30,8 +41,7 @@ def tile_picked_ypartnr_max_po_kernel(
     with ExitStack() as ctx:
         keep = ctx.enter_context(tc.tile_pool(name="keep", bufs=1))
         ring = ctx.enter_context(tc.tile_pool(name="ring", bufs=2))
-        psum1 = ctx.enter_context(tc.psum_pool(name="psum1", bufs=1))
-        psum2 = ctx.enter_context(tc.psum_pool(name="psum2", bufs=2))
+        psum = ctx.enter_context(tc.psum_pool(name="psum", bufs=1))
 
         def load_scale_rows(queues, dst, src):
             for q, queue in enumerate(queues):
@@ -42,8 +52,9 @@ def tile_picked_ypartnr_max_po_kernel(
 
         xs = keep.tile([P, PASSES, T], U8, name="xs", align_bytes=64)
         ws_raw = keep.tile([P, PASSES, H], U8, name="ws_raw", align_bytes=64)
-        nc.vector.memset(xs[:].bitcast(I32), 0)
-        nc.gpsimd.memset(ws_raw[:].bitcast(I32), 0)
+        nc.vector.memset(xs[:, 0, :].bitcast(I32), 0)
+        nc.gpsimd.memset(xs[:, 1, :].bitcast(I32), 0)
+        nc.vector.memset(ws_raw[:].bitcast(I32), 0)
 
         offs_sb = keep.tile([P, S // 16], U16, name="offs_sb")
         nc.sync.dma_start(offs_sb[:], offs)
@@ -51,15 +62,15 @@ def tile_picked_ypartnr_max_po_kernel(
         ww_raw = keep.tile([P, PASSES, 2 * H], U8, name="ww_raw", align_bytes=64)
         nc.sync.dma_start(out=ww_raw[:].bitcast(I32), in_=w1_words.bitcast(I32).rearrange("o p c -> p o c"))
         u_sb = keep.tile([P, PACK], F32, name="u_sb")
+        lists = {name: keep.tile([P, U // 16], U16, name=f"{name}_sb") for name in ("el", "nu", "ct")}
         nc.sync.dma_start(out=u_sb[:], in_=unit.rearrange("(p t) o -> p (t o)", t=PACK))
-        load_scale_rows((nc.scalar, nc.scalar, nc.gpsimd, nc.gpsimd), ws_raw[:], w1_scales)
-        load_scale_rows([nc.scalar] * 4, xs[:], x_scales)
-        for o in range(PASSES):
-            nc.sync.dma_start(out=xw[o][:], in_=x_words[o].rearrange("p c t -> p (c t)").bitcast(I32))
-        lists = {}
-        for name, src in (("el", el), ("nu", nu), ("ct", ct)):
-            lists[name] = keep.tile([P, U // 16], U16, name=f"{name}_sb")
-            nc.sync.dma_start(lists[name][:], src)
+        load_scale_rows((nc.sync, nc.scalar, nc.scalar, nc.scalar), xs[:], x_scales)
+        nc.sync.dma_start(out=xw[0][:], in_=x_words[0].rearrange("p c t -> p (c t)").bitcast(I32))
+        load_scale_rows((nc.sync, nc.sync, nc.scalar, nc.scalar), ws_raw[:], w1_scales)
+        nc.sync.dma_start(out=xw[1][:], in_=x_words[1].rearrange("p c t -> p (c t)").bitcast(I32))
+        nc.sync.dma_start(lists["el"][:], el)
+        nc.sync.dma_start(lists["nu"][:], nu)
+        nc.sync.dma_start(lists["ct"][:], ct)
 
         sign = keep.tile([P, PACK], F32, name="sign")
         nc.scalar.activation(sign[:], u_sb[:], ACT.Sign)
@@ -75,35 +86,36 @@ def tile_picked_ypartnr_max_po_kernel(
             words, scales = dealt
             return dict(lhsT=words[:, t].rearrange("p m b -> p (m b)").bitcast(FP4X4), lhsT_scale=scales[:, t, :])
 
-        y_banks = [psum1.tile([P, S], F32, name=f"y{t}") for t in range(PACK)]
+        y_banks = [psum.tile([P, S], F32, name=f"low{t}") for t in range(PACK)]
+        w1, xq = [], []
         for o in range(PASSES):
-            w1 = deal(ww_raw[:, o, :], ws_raw[:, o, :], f"w1_{o}")
             xq_s = keep.tile([P, S], U8, name=f"xq_s{o}", align_bytes=64)
             xq_w = keep.tile([P, S], U32, name=f"xq_w{o}", align_bytes=64)
+            w1.append(deal(ww_raw[:, o, :], ws_raw[:, o, :], f"w1_{o}"))
             nc.vector.tensor_copy(xq_s[:], xs[:, o, :].indirect(offs_sb[:]))
             nc.vector.tensor_copy(xq_w[:], xw[o][:].bitcast(U32).indirect(offs_sb[:]))
-            for t in range(PACK):
+            xq.append(dict(rhs=xq_w[:].bitcast(FP8X4), rhs_scale=xq_s[:]))
+        for t in range(PACK):
+            for o in range(PASSES):
                 nc.tensor.matmul_mx(
-                    out=y_banks[t][:], rhs=xq_w[:].bitcast(FP8X4), rhs_scale=xq_s[:],
-                    start=(o == 0), stop=(o == PASSES - 1), **stationary(w1, t),
+                    out=y_banks[t][:], start=(o == 0), stop=(o == PASSES - 1), **xq[o], **stationary(w1[o], t)
                 )
 
         nc.sync.dma_start(out=ww_raw[:, 0:1, :].bitcast(I32), in_=w2_words.bitcast(I32).rearrange("o p c -> p o c"))
         load_scale_rows([nc.sync] * 4, ws_raw[:, 0:1, :], w2_scales)
-        w2 = deal(ww_raw[:, 0, :], ws_raw[:, 0, :], "w2")
 
         y_signed, y_scaled = [], []
         for t in range(PACK):
-            ys = keep.tile([P, S], F32, name=f"y_signed{t}")
-            ya = keep.tile([P, S], F32, name=f"y_scaled{t}")
-            if t % 2 == 0:
-                nc.scalar.activation(ys[:], y_banks[t][:], ACT.Copy, scale=sign[:, t : t + 1])
-            else:
-                nc.vector.tensor_scalar(ys[:], y_banks[t][:], sign[:, t : t + 1], None, ALU.mult)
-            nc.vector.tensor_scalar(ya[:], ys[:], u_sb[:, t : t + 1], None, ALU.mult)
+            ys = keep.tile([P, WINDOW], F32, name=f"y_signed{t}")
+            ya = keep.tile([P, WINDOW], F32, name=f"y_scaled{t}")
+            nc.vector.memset(ys[:, S:], 0.0)
+            nc.vector.memset(ya[:, S:], 0.0)
+            nc.vector.tensor_scalar(ys[:, :S], y_banks[t][:], sign[:, t : t + 1], None, ALU.mult)
+            nc.vector.tensor_scalar(ya[:, :S], ys[:, :S], u_sb[:, t : t + 1], None, ALU.mult)
             y_signed.append(ys)
             y_scaled.append(ya)
 
+        w2 = deal(ww_raw[:, 0, :], ws_raw[:, 0, :], "w1_1")
         out_scales = keep.tile([P, U], U8, name="out_scales", align_bytes=64)
         out_rows = out_0.rearrange("(p t) r -> p t r", t=PACK)
         out_words = out_1[0].rearrange("p c t -> p (c t)").bitcast(I32)
@@ -114,65 +126,67 @@ def tile_picked_ypartnr_max_po_kernel(
         def by_rows(ap):
             return ap.rearrange("p t (c i) -> p c t i", i=4)
 
-        def hidden(r0, width):
-            cols = slice(r0 // 16, (r0 + width) // 16)
-            taker = ring.tile([P, PACK, width], F32, name="taker")
-            giver = ring.tile([P, PACK, width], F32, name="giver")
-            larger = ring.tile([P, PACK, width], F32, name="larger")
-            act = ring.tile([P, PACK, width], F32, name="act")
-            for t in range(PACK):
-                nc.scalar.activation(taker[:, t, :], y_signed[t][:].indirect(lists["el"][:, cols]), ACT.Copy)
-                nc.scalar.activation(giver[:, t, :], y_scaled[t][:].indirect(lists["nu"][:, cols]), ACT.Copy)
-            for t in range(PACK + 1):
-                if t < PACK:
-                    nc.vector.scalar_tensor_tensor(
-                        larger[:, t, :], taker[:, t, :], u_sb[:, t : t + 1], giver[:, t, :], ALU.mult, ALU.max
-                    )
-                if t > 0:
-                    nc.vector.tensor_tensor(
-                        act[:, t - 1, :], y_scaled[t - 1][:].indirect(lists["ct"][:, cols]), larger[:, t - 1, :], ALU.add
-                    )
-            hid = ring.tile([P, width, PACK], BF16, name="hid", align_bytes=64)
-            nc.vector.tensor_tensor(woven(hid[:]), by_rows(act[:]), by_rows(taker[:]), ALU.mult)
-            return hid
+        def looked_up(window, name, r0, width):
+            return window[:].indirect(lists[name][:, r0 // 16 : (r0 + width) // 16])
 
-        def second_product(hid, width):
-            codes = ring.tile([P, width], U32, name="hid_codes", align_bytes=64)
-            scales = ring.tile([P, width], U8, name="hid_scales", align_bytes=64)
+        def hidden(r0, width, fused):
+            taker = keep.tile([P, PACK, width], F32, name=f"taker{r0}")
+            act = keep.tile([P, PACK, width], F32, name=f"act{r0}")
+            for t in range(PACK):
+                giver = keep.tile([P, width], F32, name=f"giver{r0}_{t}")
+                larger = ring.tile([P, width], F32, name="larger")
+                nc.scalar.activation(taker[:, t, :], looked_up(y_signed[t], "el", r0, width), ACT.Copy)
+                if r0 == 0 and t == PACK - 1:
+                    nc.vector.tensor_copy(giver[:], looked_up(y_scaled[t], "nu", r0, width))
+                else:
+                    nc.scalar.activation(giver[:], looked_up(y_scaled[t], "nu", r0, width), ACT.Copy)
+                nc.vector.scalar_tensor_tensor(larger[:], taker[:, t, :], u_sb[:, t : t + 1], giver[:], ALU.mult, ALU.max)
+                if t < fused:
+                    nc.vector.tensor_tensor(act[:, t, :], looked_up(y_scaled[t], "ct", r0, width), larger[:], ALU.add)
+                else:
+                    catalyst = keep.tile([P, width], F32, name=f"catalyst{r0}_{t}")
+                    nc.scalar.activation(catalyst[:], looked_up(y_scaled[t], "ct", r0, width), ACT.Copy)
+                    nc.vector.tensor_tensor(act[:, t, :], catalyst[:], larger[:], ALU.add)
+            hid = ring.tile([P, width, PACK], BF16, name="woven_bf16", align_bytes=64)
+            nc.vector.tensor_tensor(woven(hid[:]), by_rows(act[:]), by_rows(taker[:]), ALU.mult)
+            codes = keep.tile([P, width], U32, name=f"hid_codes{r0}", align_bytes=64)
+            scales = keep.tile([P, width], U8, name=f"hid_scales{r0}", align_bytes=64)
             nc.vector.quantize_mx(out=codes[:].bitcast(FP8X4), scales=scales[:], in_=hid[:].rearrange("p r t -> p (r t)"))
-            res = ring.tile([P, PACK, width], F32, name="res")
+            return codes, scales
+
+        def second_product(codes, scales, r0, width, bank_tag):
+            res = keep.tile([P, PACK, width], F32, name=f"res{r0}")
             per_bank = min(BANK // width, PACK)
             for b in range(PACK // per_bank):
-                bank = psum2.tile([P, per_bank, width], F32, name=f"bank{b}")
+                bank = psum.tile([P, per_bank, width], F32, name=f"{bank_tag}{b}")
                 for j in range(per_bank):
-                    nc.tensor.matmul_mx(
-                        out=bank[:, j, :], rhs=codes[:].bitcast(FP8X4), rhs_scale=scales[:],
-                        start=True, stop=True, **stationary(w2, per_bank * b + j),
-                    )
+                    for c0, c1 in pieces(width):
+                        nc.tensor.matmul_mx(
+                            out=bank[:, j, c0:c1], rhs=codes[:, c0:c1].bitcast(FP8X4), rhs_scale=scales[:, c0:c1],
+                            start=True, stop=True, **stationary(w2, per_bank * b + j),
+                        )
                 nc.scalar.copy(res[:, per_bank * b : per_bank * (b + 1), :], bank[:])
+            nc.sync.dma_start(out=out_rows[:, :, r0 : r0 + width], in_=res[:])
             return res
 
         def hand_out(res, r0, width):
-            nc.sync.dma_start(out=out_rows[:, :, r0 : r0 + width], in_=res[:])
-            rounded = ring.tile([P, width, PACK], BF16, name="rounded", align_bytes=64)
+            rounded = ring.tile([P, width, PACK], BF16, name="woven_bf16", align_bytes=64)
             nc.vector.tensor_copy(woven(rounded[:]), by_rows(res[:]))
-            codes = ring.tile([P, width], U32, name="out_codes", align_bytes=64)
+            codes = keep.tile([P, width], U32, name=f"out_codes{r0}", align_bytes=64)
             nc.vector.quantize_mx(
                 out=codes[:].bitcast(FP8X4), scales=out_scales[:, r0 : r0 + width],
                 in_=rounded[:].rearrange("p r t -> p (r t)"),
             )
             nc.sync.dma_start(out=out_words[:, r0 : r0 + width], in_=codes[:].bitcast(I32))
 
-        waiting = None
-        r0 = 0
-        for width in WIDTHS:
-            hid = hidden(r0, width)
-            if waiting is not None:
-                hand_out(*waiting)
-            waiting = (second_product(hid, width), r0, width)
-            r0 = r0 + width
-        hand_out(*waiting)
+        starts = [sum(WIDTHS[:c]) for c in range(len(WIDTHS))]
+        quantised = [hidden(*chunk) for chunk in zip(starts, WIDTHS, FUSED)]
+        results = [
+            second_product(*quantised[c], starts[c], WIDTHS[c], ("high", "low")[c % 2]) for c in range(len(WIDTHS))
+        ]
+        for res, r0, width in zip(results, starts, WIDTHS):
+            hand_out(res, r0, width)
         for q in range(4):
-            nc.sync.dma_start(
+            (nc.sync, nc.scalar)[q % 2].dma_start(
                 out=out_2[0, 4 * q : 4 * q + 4, :].bitcast(I32), in_=out_scales[32 * q : 32 * q + 4, :].bitcast(I32)
             )

@@ -20,7 +20,7 @@ P = 128
 PACK = 4
 PASSES = K // (P * PACK)
 WIDTHS = (512, 384, 128)
-FUSED = (4, 2, 0)
+FUSED = (4, 2, 4)
 WINDOW = S + 16
 BANK = 512
 
@@ -50,11 +50,12 @@ def tile_picked_ypartnr_max_po_kernel(
                     in_=src[:, 4 * q : 4 * q + 4, :].bitcast(I32).rearrange("o r c -> r o c"),
                 )
 
-        xs = keep.tile([P, PASSES, T], U8, name="xs", align_bytes=64)
+        xs = keep.tile([P, T], U8, name="xs", align_bytes=64)
+        xq_s = [keep.tile([P, S], U8, name=f"xq_s{o}", align_bytes=64) for o in range(PASSES)]
         ws_raw = keep.tile([P, PASSES, H], U8, name="ws_raw", align_bytes=64)
-        nc.vector.memset(xs[:, 0, :].bitcast(I32), 0)
-        nc.gpsimd.memset(xs[:, 1, :].bitcast(I32), 0)
+        nc.vector.memset(xs[:].bitcast(I32), 0)
         nc.vector.memset(ws_raw[:].bitcast(I32), 0)
+        nc.vector.memset(xq_s[1][:].bitcast(I32), 0)
 
         offs_sb = keep.tile([P, S // 16], U16, name="offs_sb")
         nc.sync.dma_start(offs_sb[:], offs)
@@ -64,7 +65,8 @@ def tile_picked_ypartnr_max_po_kernel(
         u_sb = keep.tile([P, PACK], F32, name="u_sb")
         lists = {name: keep.tile([P, U // 16], U16, name=f"{name}_sb") for name in ("el", "nu", "ct")}
         nc.sync.dma_start(out=u_sb[:], in_=unit.rearrange("(p t) o -> p (t o)", t=PACK))
-        load_scale_rows((nc.sync, nc.scalar, nc.scalar, nc.scalar), xs[:], x_scales)
+        for q, queue in enumerate((nc.sync, nc.scalar, nc.scalar, nc.scalar)):
+            queue.dma_start(out=xs[32 * q : 32 * q + 8, :].bitcast(I32), in_=x_scales[:, 4 * q : 4 * q + 4, :].bitcast(I32))
         nc.sync.dma_start(out=xw[0][:], in_=x_words[0].rearrange("p c t -> p (c t)").bitcast(I32))
         load_scale_rows((nc.sync, nc.sync, nc.scalar, nc.scalar), ws_raw[:], w1_scales)
         nc.sync.dma_start(out=xw[1][:], in_=x_words[1].rearrange("p c t -> p (c t)").bitcast(I32))
@@ -75,26 +77,29 @@ def tile_picked_ypartnr_max_po_kernel(
         sign = keep.tile([P, PACK], F32, name="sign")
         nc.scalar.activation(sign[:], u_sb[:], ACT.Sign)
 
-        def deal(words_raw, scales_raw, name):
-            words = keep.tile([P, PACK, P, 2], U8, name=f"{name}_words", align_bytes=64)
-            scales = keep.tile([P, PACK, P], U8, name=f"{name}_scales", align_bytes=64)
-            nc.vector.tensor_copy(words[:], words_raw.rearrange("p (m t b) -> p t m b", t=PACK, b=2))
+        def deal(words_raw, scales_raw, name, scales_name):
+            words = keep.tile([P, PACK, P], U16, name=f"{name}_words", align_bytes=64)
+            scales = keep.tile([P, PACK, P], U8, name=scales_name, align_bytes=64)
+            nc.scalar.copy(words[:], words_raw.bitcast(U16).rearrange("p (m t) -> p t m", t=PACK))
             nc.vector.tensor_copy(scales[:], scales_raw.rearrange("p (m t) -> p t m", t=PACK))
             return words, scales
 
         def stationary(dealt, t):
             words, scales = dealt
-            return dict(lhsT=words[:, t].rearrange("p m b -> p (m b)").bitcast(FP4X4), lhsT_scale=scales[:, t, :])
+            return dict(lhsT=words[:, t, :].bitcast(FP4X4), lhsT_scale=scales[:, t, :])
 
         y_banks = [psum.tile([P, S], F32, name=f"low{t}") for t in range(PACK)]
+        nc.vector.tensor_copy(xq_s[0][:], xs[:].indirect(offs_sb[:]))
+        for q in range(4):
+            nc.scalar.dma_start(
+                out=xq_s[1][32 * q : 32 * q + 4, :].bitcast(I32), in_=xq_s[0][32 * q + 4 : 32 * q + 8, :].bitcast(I32)
+            )
         w1, xq = [], []
         for o in range(PASSES):
-            xq_s = keep.tile([P, S], U8, name=f"xq_s{o}", align_bytes=64)
             xq_w = keep.tile([P, S], U32, name=f"xq_w{o}", align_bytes=64)
-            w1.append(deal(ww_raw[:, o, :], ws_raw[:, o, :], f"w1_{o}"))
-            nc.vector.tensor_copy(xq_s[:], xs[:, o, :].indirect(offs_sb[:]))
+            w1.append(deal(ww_raw[:, o, :], ws_raw[:, o, :], f"w1_{o}", f"w1_{o}_scales"))
             nc.vector.tensor_copy(xq_w[:], xw[o][:].bitcast(U32).indirect(offs_sb[:]))
-            xq.append(dict(rhs=xq_w[:].bitcast(FP8X4), rhs_scale=xq_s[:]))
+            xq.append(dict(rhs=xq_w[:].bitcast(FP8X4), rhs_scale=xq_s[o][:]))
         for t in range(PACK):
             for o in range(PASSES):
                 nc.tensor.matmul_mx(
@@ -110,45 +115,53 @@ def tile_picked_ypartnr_max_po_kernel(
             ya = keep.tile([P, WINDOW], F32, name=f"y_scaled{t}")
             nc.vector.memset(ys[:, S:], 0.0)
             nc.vector.memset(ya[:, S:], 0.0)
-            nc.vector.tensor_scalar(ys[:, :S], y_banks[t][:], sign[:, t : t + 1], None, ALU.mult)
+            if t == 0:
+                nc.scalar.activation(ys[:, :S], y_banks[t][:], ACT.Copy, scale=sign[:, t : t + 1])
+            else:
+                nc.vector.tensor_scalar(ys[:, :S], y_banks[t][:], sign[:, t : t + 1], None, ALU.mult)
             nc.vector.tensor_scalar(ya[:, :S], ys[:, :S], u_sb[:, t : t + 1], None, ALU.mult)
             y_signed.append(ys)
             y_scaled.append(ya)
 
-        w2 = deal(ww_raw[:, 0, :], ws_raw[:, 0, :], "w1_1")
+        w2 = deal(ww_raw[:, 0, :], ws_raw[:, 0, :], "w2", "xw1")
         out_scales = keep.tile([P, U], U8, name="out_scales", align_bytes=64)
         out_rows = out_0.rearrange("(p t) r -> p t r", t=PACK)
         out_words = out_1[0].rearrange("p c t -> p (c t)").bitcast(I32)
 
         def woven(ap):
-            return ap.rearrange("p (c i) t -> p c t i", i=4)
+            return ap.rearrange("p (c i) t -> p c t i", i=2)
 
         def by_rows(ap):
-            return ap.rearrange("p t (c i) -> p c t i", i=4)
+            return ap.rearrange("p t (c i) -> p c t i", i=2)
 
         def looked_up(window, name, r0, width):
             return window[:].indirect(lists[name][:, r0 // 16 : (r0 + width) // 16])
 
         def hidden(r0, width, fused):
-            taker = keep.tile([P, PACK, width], F32, name=f"taker{r0}")
+            fetched = keep.tile([P, 2, PACK, width], F32, name=f"fetched{r0}")
+            if fused < PACK:
+                catalysts = keep.tile(
+                    [P, PACK, width], F32, name="hid_codes0" if r0 + width == U else f"catalysts{r0}", align_bytes=64
+                )
+            taker = fetched[:, 0]
             act = keep.tile([P, PACK, width], F32, name=f"act{r0}")
             for t in range(PACK):
-                giver = keep.tile([P, width], F32, name=f"giver{r0}_{t}")
+                giver = fetched[:, 1, t, :]
                 larger = ring.tile([P, width], F32, name="larger")
                 nc.scalar.activation(taker[:, t, :], looked_up(y_signed[t], "el", r0, width), ACT.Copy)
                 if r0 == 0 and t == PACK - 1:
-                    nc.vector.tensor_copy(giver[:], looked_up(y_scaled[t], "nu", r0, width))
+                    nc.vector.tensor_copy(giver, looked_up(y_scaled[t], "nu", r0, width))
                 else:
-                    nc.scalar.activation(giver[:], looked_up(y_scaled[t], "nu", r0, width), ACT.Copy)
-                nc.vector.scalar_tensor_tensor(larger[:], taker[:, t, :], u_sb[:, t : t + 1], giver[:], ALU.mult, ALU.max)
+                    nc.scalar.activation(giver, looked_up(y_scaled[t], "nu", r0, width), ACT.Copy)
+                nc.vector.scalar_tensor_tensor(larger[:], taker[:, t, :], u_sb[:, t : t + 1], giver, ALU.mult, ALU.max)
                 if t < fused:
                     nc.vector.tensor_tensor(act[:, t, :], looked_up(y_scaled[t], "ct", r0, width), larger[:], ALU.add)
                 else:
-                    catalyst = keep.tile([P, width], F32, name=f"catalyst{r0}_{t}")
-                    nc.scalar.activation(catalyst[:], looked_up(y_scaled[t], "ct", r0, width), ACT.Copy)
-                    nc.vector.tensor_tensor(act[:, t, :], catalyst[:], larger[:], ALU.add)
+                    catalyst = catalysts[:, t, :]
+                    nc.scalar.activation(catalyst, looked_up(y_scaled[t], "ct", r0, width), ACT.Copy)
+                    nc.vector.tensor_tensor(act[:, t, :], catalyst, larger[:], ALU.add)
             hid = ring.tile([P, width, PACK], BF16, name="woven_bf16", align_bytes=64)
-            nc.vector.tensor_tensor(woven(hid[:]), by_rows(act[:]), by_rows(taker[:]), ALU.mult)
+            nc.vector.tensor_tensor(woven(hid[:]), by_rows(act[:]), by_rows(taker), ALU.mult)
             codes = keep.tile([P, width], U32, name=f"hid_codes{r0}", align_bytes=64)
             scales = keep.tile([P, width], U8, name=f"hid_scales{r0}", align_bytes=64)
             nc.vector.quantize_mx(out=codes[:].bitcast(FP8X4), scales=scales[:], in_=hid[:].rearrange("p r t -> p (r t)"))
@@ -180,10 +193,13 @@ def tile_picked_ypartnr_max_po_kernel(
             nc.sync.dma_start(out=out_words[:, r0 : r0 + width], in_=codes[:].bitcast(I32))
 
         starts = [sum(WIDTHS[:c]) for c in range(len(WIDTHS))]
-        quantised = [hidden(*chunk) for chunk in zip(starts, WIDTHS, FUSED)]
-        results = [
-            second_product(*quantised[c], starts[c], WIDTHS[c], ("high", "low")[c % 2]) for c in range(len(WIDTHS))
-        ]
+        first, second, last = zip(starts, WIDTHS, FUSED)
+        hid_first = hidden(*first)
+        hid_second = hidden(*second)
+        results = [second_product(*hid_first, *first[:2], "high")]
+        hid_last = hidden(*last)
+        results.append(second_product(*hid_second, *second[:2], "low"))
+        results.append(second_product(*hid_last, *last[:2], "high"))
         for res, r0, width in zip(results, starts, WIDTHS):
             hand_out(res, r0, width)
         for q in range(4):

from contextlib import ExitStack

import concourse.mybir as mybir

K, T, S, H, N, U = 1024, 2048, 512, 512, 512, 1024
FLOPS = 2 * K * H * S + 2 * H * N * U

F32 = mybir.dt.float32
BF16 = mybir.dt.bfloat16
I32 = mybir.dt.int32
U32 = mybir.dt.uint32
U16 = mybir.dt.uint16
U8 = mybir.dt.uint8
FP8X4 = mybir.dt.float8_e4m3fn_x4
FP4X4 = mybir.dt.float4_e2m1fn_x4
ALU = mybir.AluOpType
ACT = mybir.ActivationFunctionType

P = 128
PACK = 4
PASSES = K // (P * PACK)
WIDTHS = (512, 384, 128)
FUSED = (4, 2, 4)
WINDOW = S + 16
BANK = 512


def pieces(width):
    cuts, c0 = [], 0
    for n in (512, 256, 128):
        if width - c0 >= n:
            cuts.append((c0, c0 + n))
            c0 = c0 + n
    return cuts


def tile_picked_ypartnr_max_po_kernel(
    tc, x_words, x_scales, w1_words, w1_scales, unit, w2_words, w2_scales, offs, nu, el, ct, out_0, out_1, out_2
):
    nc = tc.nc
    with ExitStack() as ctx:
        keep = ctx.enter_context(tc.tile_pool(name="keep", bufs=1))
        ring = ctx.enter_context(tc.tile_pool(name="ring", bufs=2))
        psum = ctx.enter_context(tc.psum_pool(name="psum", bufs=1))

        def load_scale_rows(queues, dst, src):
            for q, queue in enumerate(queues):
                queue.dma_start(
                    out=dst[32 * q : 32 * q + 4].bitcast(I32),
                    in_=src[:, 4 * q : 4 * q + 4, :].bitcast(I32).rearrange("o r c -> r o c"),
                )

        xs = keep.tile([P, T], U8, name="xs", align_bytes=64)
        xq_s = [keep.tile([P, S], U8, name=f"xq_s{o}", align_bytes=64) for o in range(PASSES)]
        ws_raw = keep.tile([P, PASSES, H], U8, name="ws_raw", align_bytes=64)
        nc.vector.memset(xs[:].bitcast(I32), 0)
        nc.vector.memset(ws_raw[:].bitcast(I32), 0)
        nc.vector.memset(xq_s[1][:].bitcast(I32), 0)

        offs_sb = keep.tile([P, S // 16], U16, name="offs_sb")
        nc.sync.dma_start(offs_sb[:], offs)
        xw = [keep.tile([P, T], I32, name=f"xw{o}", align_bytes=64) for o in range(PASSES)]
        ww_raw = keep.tile([P, PASSES, 2 * H], U8, name="ww_raw", align_bytes=64)
        nc.sync.dma_start(out=ww_raw[:].bitcast(I32), in_=w1_words.bitcast(I32).rearrange("o p c -> p o c"))
        u_sb = keep.tile([P, PACK], F32, name="u_sb")
        lists = {name: keep.tile([P, U // 16], U16, name=f"{name}_sb") for name in ("el", "nu", "ct")}
        nc.sync.dma_start(out=u_sb[:], in_=unit.rearrange("(p t) o -> p (t o)", t=PACK))
        for q, queue in enumerate((nc.sync, nc.scalar, nc.scalar, nc.scalar)):
            queue.dma_start(out=xs[32 * q : 32 * q + 8, :].bitcast(I32), in_=x_scales[:, 4 * q : 4 * q + 4, :].bitcast(I32))
        nc.sync.dma_start(out=xw[0][:], in_=x_words[0].rearrange("p c t -> p (c t)").bitcast(I32))
        load_scale_rows((nc.sync, nc.sync, nc.scalar, nc.scalar), ws_raw[:], w1_scales)
        nc.sync.dma_start(out=xw[1][:], in_=x_words[1].rearrange("p c t -> p (c t)").bitcast(I32))
        nc.sync.dma_start(lists["el"][:], el)
        nc.sync.dma_start(lists["nu"][:], nu)
        nc.sync.dma_start(lists["ct"][:], ct)

        sign = keep.tile([P, PACK], F32, name="sign")
        nc.scalar.activation(sign[:], u_sb[:], ACT.Sign)

        def deal(words_raw, scales_raw, name, scales_name):
            words = keep.tile([P, PACK, P], U16, name=f"{name}_words", align_bytes=64)
            scales = keep.tile([P, PACK, P], U8, name=scales_name, align_bytes=64)
            nc.scalar.copy(words[:], words_raw.bitcast(U16).rearrange("p (m t) -> p t m", t=PACK))
            nc.vector.tensor_copy(scales[:], scales_raw.rearrange("p (m t) -> p t m", t=PACK))
            return words, scales

        def stationary(dealt, t):
            words, scales = dealt
            return dict(lhsT=words[:, t, :].bitcast(FP4X4), lhsT_scale=scales[:, t, :])

        y_banks = [psum.tile([P, S], F32, name=f"low{t}") for t in range(PACK)]
        nc.vector.tensor_copy(xq_s[0][:], xs[:].indirect(offs_sb[:]))
        for q in range(4):
            nc.scalar.dma_start(
                out=xq_s[1][32 * q : 32 * q + 4, :].bitcast(I32), in_=xq_s[0][32 * q + 4 : 32 * q + 8, :].bitcast(I32)
            )
        w1, xq = [], []
        for o in range(PASSES):
            xq_w = keep.tile([P, S], U32, name=f"xq_w{o}", align_bytes=64)
            w1.append(deal(ww_raw[:, o, :], ws_raw[:, o, :], f"w1_{o}", f"w1_{o}_scales"))
            nc.vector.tensor_copy(xq_w[:], xw[o][:].bitcast(U32).indirect(offs_sb[:]))
            xq.append(dict(rhs=xq_w[:].bitcast(FP8X4), rhs_scale=xq_s[o][:]))
        for t in range(PACK):
            for o in range(PASSES):
                nc.tensor.matmul_mx(
                    out=y_banks[t][:], start=(o == 0), stop=(o == PASSES - 1), **xq[o], **stationary(w1[o], t)
                )

        nc.sync.dma_start(out=ww_raw[:, 0:1, :].bitcast(I32), in_=w2_words.bitcast(I32).rearrange("o p c -> p o c"))
        load_scale_rows([nc.sync] * 4, ws_raw[:, 0:1, :], w2_scales)

        y_signed, y_scaled = [], []
        for t in range(PACK):
            ys = keep.tile([P, WINDOW], F32, name=f"y_signed{t}")
            ya = keep.tile([P, WINDOW], F32, name=f"y_scaled{t}")
            nc.vector.memset(ys[:, S:], 0.0)
            nc.vector.memset(ya[:, S:], 0.0)
            if t == 0:
                nc.scalar.activation(ys[:, :S], y_banks[t][:], ACT.Copy, scale=sign[:, t : t + 1])
            else:
                nc.vector.tensor_scalar(ys[:, :S], y_banks[t][:], sign[:, t : t + 1], None, ALU.mult)
            nc.vector.tensor_scalar(ya[:, :S], ys[:, :S], u_sb[:, t : t + 1], None, ALU.mult)
            y_signed.append(ys)
            y_scaled.append(ya)

        w2 = deal(ww_raw[:, 0, :], ws_raw[:, 0, :], "w2", "xw1")
        out_scales = keep.tile([P, U], U8, name="out_scales", align_bytes=64)
        out_rows = out_0.rearrange("(p t) r -> p t r", t=PACK)
        out_words = out_1[0].rearrange("p c t -> p (c t)").bitcast(I32)

        def woven(ap):
            return ap.rearrange("p (c i) t -> p c t i", i=2)

        def by_rows(ap):
            return ap.rearrange("p t (c i) -> p c t i", i=2)

        def looked_up(window, name, r0, width):
            return window[:].indirect(lists[name][:, r0 // 16 : (r0 + width) // 16])

        def hidden(r0, width, fused):
            fetched = keep.tile([P, 2, PACK, width], F32, name=f"fetched{r0}")
            if fused < PACK:
                catalysts = keep.tile(
                    [P, PACK, width], F32, name="hid_codes0" if r0 + width == U else f"catalysts{r0}", align_bytes=64
                )
            taker = fetched[:, 0]
            act = keep.tile([P, PACK, width], F32, name=f"act{r0}")
            for t in range(PACK):
                giver = fetched[:, 1, t, :]
                larger = ring.tile([P, width], F32, name="larger")
                nc.scalar.activation(taker[:, t, :], looked_up(y_signed[t], "el", r0, width), ACT.Copy)
                if r0 == 0 and t == PACK - 1:
                    nc.vector.tensor_copy(giver, looked_up(y_scaled[t], "nu", r0, width))
                else:
                    nc.scalar.activation(giver, looked_up(y_scaled[t], "nu", r0, width), ACT.Copy)
                nc.vector.scalar_tensor_tensor(larger[:], taker[:, t, :], u_sb[:, t : t + 1], giver, ALU.mult, ALU.max)
                if t < fused:
                    nc.vector.tensor_tensor(act[:, t, :], looked_up(y_scaled[t], "ct", r0, width), larger[:], ALU.add)
                else:
                    catalyst = catalysts[:, t, :]
                    nc.scalar.activation(catalyst, looked_up(y_scaled[t], "ct", r0, width), ACT.Copy)
                    nc.vector.tensor_tensor(act[:, t, :], catalyst, larger[:], ALU.add)
            hid = ring.tile([P, width, PACK], BF16, name="woven_bf16", align_bytes=64)
            nc.vector.tensor_tensor(woven(hid[:]), by_rows(act[:]), by_rows(taker), ALU.mult)
            codes = keep.tile([P, width], U32, name=f"hid_codes{r0}", align_bytes=64)
            scales = keep.tile([P, width], U8, name=f"hid_scales{r0}", align_bytes=64)
            nc.vector.quantize_mx(out=codes[:].bitcast(FP8X4), scales=scales[:], in_=hid[:].rearrange("p r t -> p (r t)"))
            return codes, scales

        def second_product(codes, scales, r0, width, bank_tag):
            res = keep.tile([P, PACK, width], F32, name=f"res{r0}")
            per_bank = min(BANK // width, PACK)
            for b in range(PACK // per_bank):
                bank = psum.tile([P, per_bank, width], F32, name=f"{bank_tag}{b}")
                for j in range(per_bank):
                    for c0, c1 in pieces(width):
                        nc.tensor.matmul_mx(
                            out=bank[:, j, c0:c1], rhs=codes[:, c0:c1].bitcast(FP8X4), rhs_scale=scales[:, c0:c1],
                            start=True, stop=True, **stationary(w2, per_bank * b + j),
                        )
                nc.scalar.copy(res[:, per_bank * b : per_bank * (b + 1), :], bank[:])
            nc.sync.dma_start(out=out_rows[:, :, r0 : r0 + width], in_=res[:])
            return res

        def hand_out(res, r0, width):
            rounded = ring.tile([P, width, PACK], BF16, name="woven_bf16", align_bytes=64)
            nc.vector.tensor_copy(woven(rounded[:]), by_rows(res[:]))
            codes = keep.tile([P, width], U32, name=f"out_codes{r0}", align_bytes=64)
            nc.vector.quantize_mx(
                out=codes[:].bitcast(FP8X4), scales=out_scales[:, r0 : r0 + width],
                in_=rounded[:].rearrange("p r t -> p (r t)"),
            )
            nc.sync.dma_start(out=out_words[:, r0 : r0 + width], in_=codes[:].bitcast(I32))

        starts = [sum(WIDTHS[:c]) for c in range(len(WIDTHS))]
        first, second, last = zip(starts, WIDTHS, FUSED)
        hid_first = hidden(*first)
        hid_second = hidden(*second)
        results = [second_product(*hid_first, *first[:2], "high")]
        hid_last = hidden(*last)
        results.append(second_product(*hid_second, *second[:2], "low"))
        results.append(second_product(*hid_last, *last[:2], "high"))
        for res, r0, width in zip(results, starts, WIDTHS):
            hand_out(res, r0, width)
        for q in range(4):
            (nc.sync, nc.scalar)[q % 2].dma_start(
                out=out_2[0, 4 * q : 4 * q + 4, :].bitcast(I32), in_=out_scales[32 * q : 32 * q + 4, :].bitcast(I32)
            )
